import numpy as np
import ml_dtypes


def mxq(x, axis, fmt="e4m3"):
    dtype, down = {"e4m3": (ml_dtypes.float8_e4m3fn, 7), "e5m2": (ml_dtypes.float8_e5m2, 14)}[fmt]
    v = np.moveaxis(np.asarray(x, np.float32).astype(ml_dtypes.bfloat16).astype(np.float64), axis, -1)
    blocks = v.reshape(v.shape[:-1] + (-1, 32))
    amax = np.abs(blocks).max(-1, keepdims=True)
    byte = np.maximum(np.where(amax > 0, np.frexp(amax)[1] - 1 + 127, 0) - down, 1)
    scale = np.exp2(byte - 127.0)
    codes = (blocks / scale).astype(np.float32).astype(dtype).astype(np.float64)
    return np.moveaxis((codes * scale).reshape(v.shape), -1, axis)


WIDE = False


def mx_kscale(k):
    if not WIDE:
        return np.ones(k)
    levels = np.array([10, -10, 5, -5, 0])
    if k % 512:
        return np.exp2(np.random.permutation(np.resize(levels, k // 32))).repeat(32)
    a = np.empty((k // 512, 16))
    for p in range(k // 512):
        a[p, :8] = np.random.permutation(np.resize(levels, 8))
        for g in range(8):
            far = levels[np.abs(levels - a[p, g]) >= 10]
            a[p, g + 8] = far[np.random.randint(len(far))]
    return np.exp2(a.ravel()).repeat(32)


def f64(x):
    return np.asarray(x).astype(np.float64)


def striped8(idx):
    return np.asarray(idx).reshape(8, -1, 16).transpose(0, 2, 1).reshape(128, -1).astype(np.uint16)


def unstriped8(offs):
    return offs.reshape(8, 16, -1).transpose(0, 2, 1).reshape(8, -1).astype(np.int64)


def pick8(x, idx, run):
    r = np.arange(len(x))
    return x[r[:, None], idx[r % (8 * run) // run]]


E2M1 = np.array([0.0, 0.5, 1.0, 1.5, 2.0, 3.0, 4.0, 6.0, -0.0, -0.5, -1.0, -1.5, -2.0, -3.0, -4.0, -6.0])


def pack_weight(w, fmt):
    k, n = w.shape
    w = f64(np.asarray(w, np.float32).astype(ml_dtypes.bfloat16)).reshape(k // 32, 32, n)
    amax = np.abs(w).max(1)
    if fmt == "e4m3":
        byte = np.frexp(amax)[1] - 1 + 127 - 7
    else:
        mant, ex = np.frexp(amax / 6.0)
        byte = np.where(mant > 0.5, ex, ex - 1) + 127
    byte = np.clip(np.where(amax > 0, byte, 1), 1, 254)
    scaled = (w * np.exp2(127.0 - byte)[:, None, :]).reshape(k, n).astype(np.float32)
    by_word = np.ascontiguousarray(scaled.reshape(k // 512, 128, 4, n).transpose(0, 1, 3, 2))
    if fmt == "e4m3":
        words = by_word.astype(ml_dtypes.float8_e4m3fn).view(np.uint8)
    else:
        c = by_word.astype(ml_dtypes.float4_e2m1fn).view(np.uint8) & 0xF
        words = (c[..., 0::2] | (c[..., 1::2] << 4)).reshape(k // 512, 128, 2 * n)
    return np.ascontiguousarray(words), np.ascontiguousarray(byte.astype(np.uint8).reshape(k // 512, 16, n))


def unpack_weight(words, scales, fmt):
    g, _, n = scales.shape
    words = np.ascontiguousarray(words).reshape(g, 128, n, -1)
    if fmt == "e4m3":
        vals = words.view(ml_dtypes.float8_e4m3fn).astype(np.float64)
    else:
        nib = np.empty((g, 128, n, 4), np.uint8)
        nib[..., 0::2] = words & 0xF
        nib[..., 1::2] = words >> 4
        vals = E2M1[nib]
    vals = vals * np.repeat(np.exp2(scales.astype(np.float64) - 127.0), 8, axis=1)[..., None]
    return vals.transpose(0, 1, 3, 2).reshape(g * 512, n)


D, T, U, I, Q = 512, 1024, 1024, 512, 128


def setup_inputs():
    n = np.random.standard_normal
    idx = np.stack([np.random.permutation(T)[:I] for _ in range(8)])
    idx2 = np.stack([np.random.permutation(U)[:I] for _ in range(8)])
    idx3 = np.stack([np.random.permutation(T)[:I] for _ in range(8)])
    idx4 = np.stack([np.random.permutation(U)[:I] for _ in range(8)])
    idx5 = np.stack([np.random.permutation(T)[:I] for _ in range(8)])
    fd = mx_kscale(D)
    cachep = pack_weight(n((D, T)) / fd[:, None], "e2m1")
    draftp = pack_weight(n((D, U)) / fd[:, None], "e4m3")
    return {
        "query": (n((D, Q)) * 1.0 / np.sqrt(D) * fd[:, None]).astype(np.float32),
        "cache_words": cachep[0],
        "cache_scales": cachep[1],
        "draft_words": draftp[0],
        "draft_scales": draftp[1],
        "offs": striped8(idx),
        "offs2": striped8(idx2),
        "offs3": striped8(idx3),
        "offs4": striped8(idx4),
        "offs5": striped8(idx5),
    }


def reference(query, cache_words, cache_scales, draft_words, draft_scales, offs, offs2, offs3, offs4, offs5):
    idx = unstriped8(offs)
    idx2 = unstriped8(offs2)
    idx3 = unstriped8(offs3)
    idx4 = unstriped8(offs4)
    idx5 = unstriped8(offs5)
    cacheu = unpack_weight(cache_words, cache_scales, "e2m1")
    draftu = unpack_weight(draft_words, draft_scales, "e4m3")
    queryq = mxq(f64(query), 0, "e4m3")
    a = queryq.T @ cacheu
    b = queryq.T @ draftu
    f1 = np.zeros((Q, U))
    f1[np.arange(Q)[:, None], idx2[np.arange(Q) % 128 // 16]] = pick8(a, idx, 16)
    f2 = np.zeros((Q, T))
    f2[np.arange(Q)[:, None], idx[np.arange(Q) % 128 // 16]] = pick8(b, idx2, 16)
    aa = np.maximum(a, f2)
    bb = b - f1
    f3 = np.zeros((Q, T))
    f3[np.arange(Q)[:, None], idx3[np.arange(Q) % 128 // 16]] = pick8(bb, idx4, 16)
    ac = aa + f3
    y = pick8(ac, idx5, 16)
    return y

@@ -1,0 +1,143 @@
+from contextlib import ExitStack
+
+import concourse.mybir as mybir
+
+D, T, U, SLOTS, Q = 512, 1024, 1024, 512, 128
+FLOPS = 2 * D * Q * (T + U)
+
+F32 = mybir.dt.float32
+BF16 = mybir.dt.bfloat16
+I32 = mybir.dt.int32
+U32 = mybir.dt.uint32
+U16 = mybir.dt.uint16
+U8 = mybir.dt.uint8
+FP8X4 = mybir.dt.float8_e4m3fn_x4
+FP4X4 = mybir.dt.float4_e2m1fn_x4
+COPY = mybir.ActivationFunctionType.Copy
+ALU = mybir.AluOpType
+
+P = 128
+PACK = 4
+LIST_COLS = SLOTS // 16
+HALF = SLOTS // 2
+A_COLS = 256
+B_COLS = 512
+
+
+def tile_attend_mutualput_two_kernel(
+    tc, query, cache_words, cache_scales, draft_words, draft_scales, offs, offs2, offs3, offs4, offs5, out
+):
+    nc = tc.nc
+    with ExitStack() as ctx:
+        sb = ctx.enter_context(tc.tile_pool(name="sb", bufs=1))
+        ps = ctx.enter_context(tc.psum_pool(name="ps", bufs=1))
+
+        def load_list(source, name):
+            tile = sb.tile([P, LIST_COLS], U16, name=name)
+            nc.sync.dma_start(tile[:], source)
+            return tile
+
+        def half_of(list_tile, h):
+            return list_tile[:, h * LIST_COLS // 2 : (h + 1) * LIST_COLS // 2]
+
+        def load_scales(queue, plane, source):
+            rows = source[0].bitcast(I32)
+            for quadrant in range(4):
+                queue.dma_start(
+                    plane[32 * quadrant : 32 * quadrant + 4, :].bitcast(I32), rows[4 * quadrant : 4 * quadrant + 4, :]
+                )
+
+        cache_plane = sb.tile([P, T], U8, align_bytes=64)
+        draft_plane = sb.tile([P, U], U8, align_bytes=64)
+        nc.vector.memset(cache_plane[:].bitcast(I32), 0)
+
+        q_raw = sb.tile([P, PACK, Q], F32)
+        nc.sync.dma_start(q_raw[:], query.rearrange("(p j) q -> p j q", j=PACK))
+        load_scales(nc.scalar, cache_plane, cache_scales)
+        cache_codes = sb.tile([P, 2 * T], U8, align_bytes=64)
+        nc.sync.dma_start(cache_codes[:].bitcast(I32), cache_words[0].bitcast(I32))
+        idx = load_list(offs, "idx")
+        idx2 = load_list(offs2, "idx2")
+
+        nc.vector.memset(draft_plane[:].bitcast(I32), 0)
+        draft_codes = sb.tile([P, U], U32, align_bytes=64)
+        nc.sync.dma_start(draft_codes[:].bitcast(I32), draft_words[0].rearrange("p n t -> p (n t)").bitcast(I32))
+        load_scales(nc.sync, draft_plane, draft_scales)
+        idx4 = load_list(offs4, "idx4")
+        idx3 = load_list(offs3, "idx3")
+        idx5 = load_list(offs5, "idx5")
+
+        f1 = sb.tile([P, U], F32)
+        f2 = sb.tile([P, T], F32)
+        for window in (f1, f2):
+            nc.vector.memset(window[:].bitcast(I32), 0)
+
+        q_bf = sb.tile([P, Q, PACK], BF16, align_bytes=64)
+        nc.vector.tensor_copy(
+            q_bf[:].rearrange("p (c i) j -> p c j i", i=4), q_raw[:].rearrange("p j (c i) -> p c j i", i=4)
+        )
+        q_codes = sb.tile([P, Q], U32, align_bytes=64)
+        q_plane = sb.tile([P, Q], U8, align_bytes=64)
+        nc.vector.quantize_mx(q_codes[:].bitcast(FP8X4), q_plane[:], q_bf[:].rearrange("p q j -> p (q j)"))
+
+        a = sb.tile([P, T], F32)
+        for piece in range(T // A_COLS):
+            cols = slice(piece * A_COLS, (piece + 1) * A_COLS)
+            bank = ps.tile([P, A_COLS], F32, name=f"a_bank{piece}")
+            nc.tensor.matmul_mx(
+                bank[:],
+                lhsT=q_codes[:].bitcast(FP8X4),
+                lhsT_scale=q_plane[:],
+                rhs=cache_codes[:, 2 * cols.start : 2 * cols.stop].bitcast(FP4X4),
+                rhs_scale=cache_plane[:, cols],
+                start=True,
+                stop=True,
+            )
+            if piece % 2 == 0:
+                nc.scalar.activation(a[:, cols], bank[:], COPY)
+            else:
+                nc.vector.tensor_copy(a[:, cols], bank[:])
+
+        for h in range(2):
+            picked_a = sb.tile([P, HALF], F32, name=f"picked_a{h}")
+            nc.vector.tensor_copy(picked_a[:], a[:].indirect(half_of(idx, h)))
+            nc.scalar.activation(f1[:].indirect(half_of(idx2, h)), picked_a[:], COPY)
+
+        b = sb.tile([P, U], F32, tag="b_then_f3")
+        for piece in range(U // B_COLS):
+            cols = slice(piece * B_COLS, (piece + 1) * B_COLS)
+            bank = ps.tile([P, B_COLS], F32, name=f"b_bank{piece}")
+            nc.tensor.matmul_mx(
+                bank[:],
+                lhsT=q_codes[:].bitcast(FP8X4),
+                lhsT_scale=q_plane[:],
+                rhs=draft_codes[:, cols].bitcast(FP8X4),
+                rhs_scale=draft_plane[:, cols],
+                start=True,
+                stop=True,
+            )
+            nc.vector.tensor_copy(b[:, cols], bank[:])
+
+        picked_b = sb.tile([P, SLOTS], F32)
+        nc.vector.tensor_copy(picked_b[:], b[:].indirect(idx2[:]))
+        nc.scalar.activation(f2[:].indirect(idx[:]), picked_b[:], COPY)
+
+        bb = sb.tile([P, U], F32)
+        nc.vector.tensor_tensor(bb[:], b[:], f1[:], ALU.subtract)
+        picked_bb = sb.tile([P, SLOTS], F32)
+        nc.vector.tensor_copy(picked_bb[:], bb[:].indirect(idx4[:]))
+        f3 = sb.tile([P, T], F32, tag="b_then_f3")
+        nc.vector.memset(f3[:].bitcast(I32), 0)
+        nc.scalar.activation(f3[:].indirect(idx3[:]), picked_bb[:], COPY)
+
+        aa = sb.tile([P, T], F32)
+        nc.vector.tensor_tensor(aa[:], a[:], f2[:], ALU.max)
+        ac = sb.tile([P, T], F32)
+        nc.vector.tensor_tensor(ac[:], aa[:], f3[:], ALU.add)
+
+        y0 = sb.tile([P, HALF], F32)
+        nc.vector.tensor_copy(y0[:], ac[:].indirect(half_of(idx5, 0)))
+        nc.sync.dma_start(out[:, 0:HALF], y0[:])
+        y1 = sb.tile([P, HALF], F32)
+        nc.scalar.activation(y1[:], ac[:].indirect(half_of(idx5, 1)), COPY)
+        nc.scalar.dma_start(out[:, HALF:SLOTS], y1[:])

@@ -20,8 +20,9 @@ P = 128
 PACK = 4
 LIST_COLS = SLOTS // 16
 HALF = SLOTS // 2
-A_COLS = 256
+A_WIDTHS = (256, 256, 256, 128, 128)
 B_COLS = 512
+CAST_SPLIT = 22
 
 
 def tile_attend_mutualput_two_kernel(
@@ -53,15 +54,17 @@ def tile_attend_mutualput_two_kernel(
 
         q_raw = sb.tile([P, PACK, Q], F32)
         nc.sync.dma_start(q_raw[:], query.rearrange("(p j) q -> p j q", j=PACK))
-        load_scales(nc.scalar, cache_plane, cache_scales)
-        cache_codes = sb.tile([P, 2 * T], U8, align_bytes=64)
-        nc.sync.dma_start(cache_codes[:].bitcast(I32), cache_words[0].bitcast(I32))
+        load_scales(nc.sync, cache_plane, cache_scales)
+        cache_halves = []
+        for h in range(2):
+            codes = sb.tile([P, T], U8, align_bytes=64, name=f"cache_codes{h}")
+            nc.sync.dma_start(codes[:].bitcast(I32), cache_words[0][:, h * T : (h + 1) * T].bitcast(I32))
+            cache_halves.append(codes)
+        draft_codes = sb.tile([P, U], U32, align_bytes=64, tag="draft_then_f3")
+        nc.sync.dma_start(draft_codes[:].bitcast(I32), draft_words[0].rearrange("p n t -> p (n t)").bitcast(I32))
         idx = load_list(offs, "idx")
         idx2 = load_list(offs2, "idx2")
-
         nc.vector.memset(draft_plane[:].bitcast(I32), 0)
-        draft_codes = sb.tile([P, U], U32, align_bytes=64)
-        nc.sync.dma_start(draft_codes[:].bitcast(I32), draft_words[0].rearrange("p n t -> p (n t)").bitcast(I32))
         load_scales(nc.sync, draft_plane, draft_scales)
         idx4 = load_list(offs4, "idx4")
         idx3 = load_list(offs3, "idx3")
@@ -73,22 +76,23 @@ def tile_attend_mutualput_two_kernel(
             nc.vector.memset(window[:].bitcast(I32), 0)
 
         q_bf = sb.tile([P, Q, PACK], BF16, align_bytes=64)
-        nc.vector.tensor_copy(
-            q_bf[:].rearrange("p (c i) j -> p c j i", i=4), q_raw[:].rearrange("p j (c i) -> p c j i", i=4)
-        )
+        woven = q_bf[:].rearrange("p (c i) j -> p c j i", i=4)
+        planar = q_raw[:].rearrange("p j (c i) -> p c j i", i=4)
+        nc.vector.tensor_copy(woven[:, 0:CAST_SPLIT], planar[:, 0:CAST_SPLIT])
+        nc.scalar.activation(woven[:, CAST_SPLIT:], planar[:, CAST_SPLIT:], COPY)
         q_codes = sb.tile([P, Q], U32, align_bytes=64)
         q_plane = sb.tile([P, Q], U8, align_bytes=64)
         nc.vector.quantize_mx(q_codes[:].bitcast(FP8X4), q_plane[:], q_bf[:].rearrange("p q j -> p (q j)"))
 
         a = sb.tile([P, T], F32)
-        for piece in range(T // A_COLS):
-            cols = slice(piece * A_COLS, (piece + 1) * A_COLS)
-            bank = ps.tile([P, A_COLS], F32, name=f"a_bank{piece}")
+        for piece, width in enumerate(A_WIDTHS):
+            cols = slice(sum(A_WIDTHS[:piece]), sum(A_WIDTHS[: piece + 1]))
+            bank = ps.tile([P, width], F32, name=f"a_bank{piece}")
             nc.tensor.matmul_mx(
                 bank[:],
                 lhsT=q_codes[:].bitcast(FP8X4),
                 lhsT_scale=q_plane[:],
-                rhs=cache_codes[:, 2 * cols.start : 2 * cols.stop].bitcast(FP4X4),
+                rhs=cache_halves[cols.start // 512][:, 2 * (cols.start % 512) : 2 * (cols.start % 512 + width)].bitcast(FP4X4),
                 rhs_scale=cache_plane[:, cols],
                 start=True,
                 stop=True,
@@ -98,12 +102,12 @@ def tile_attend_mutualput_two_kernel(
             else:
                 nc.vector.tensor_copy(a[:, cols], bank[:])
 
-        for h in range(2):
-            picked_a = sb.tile([P, HALF], F32, name=f"picked_a{h}")
-            nc.vector.tensor_copy(picked_a[:], a[:].indirect(half_of(idx, h)))
-            nc.scalar.activation(f1[:].indirect(half_of(idx2, h)), picked_a[:], COPY)
+        picked_a = sb.tile([P, SLOTS], F32)
+        nc.vector.tensor_copy(picked_a[:, 0:HALF], a[:].indirect(half_of(idx, 0)))
+        nc.scalar.activation(picked_a[:, HALF:SLOTS], a[:].indirect(half_of(idx, 1)), COPY)
+        nc.scalar.activation(f1[:].indirect(idx2[:]), picked_a[:], COPY)
 
-        b = sb.tile([P, U], F32, tag="b_then_f3")
+        b = sb.tile([P, U], F32)
         for piece in range(U // B_COLS):
             cols = slice(piece * B_COLS, (piece + 1) * B_COLS)
             bank = ps.tile([P, B_COLS], F32, name=f"b_bank{piece}")
@@ -122,15 +126,15 @@ def tile_attend_mutualput_two_kernel(
         nc.vector.tensor_copy(picked_b[:], b[:].indirect(idx2[:]))
         nc.scalar.activation(f2[:].indirect(idx[:]), picked_b[:], COPY)
 
-        bb = sb.tile([P, U], F32)
+        f3 = sb.tile([P, T], F32, align_bytes=64, tag="draft_then_f3")
+        nc.gpsimd.memset(f3[:].bitcast(I32), 0)
+        bb = sb.tile([P, U], F32, tag="bb_then_aa")
         nc.vector.tensor_tensor(bb[:], b[:], f1[:], ALU.subtract)
         picked_bb = sb.tile([P, SLOTS], F32)
         nc.vector.tensor_copy(picked_bb[:], bb[:].indirect(idx4[:]))
-        f3 = sb.tile([P, T], F32, tag="b_then_f3")
-        nc.vector.memset(f3[:].bitcast(I32), 0)
         nc.scalar.activation(f3[:].indirect(idx3[:]), picked_bb[:], COPY)
 
-        aa = sb.tile([P, T], F32)
+        aa = sb.tile([P, T], F32, tag="bb_then_aa")
         nc.vector.tensor_tensor(aa[:], a[:], f2[:], ALU.max)
         ac = sb.tile([P, T], F32)
         nc.vector.tensor_tensor(ac[:], aa[:], f3[:], ALU.add)

from contextlib import ExitStack

import concourse.mybir as mybir

D, T, U, SLOTS, Q = 512, 1024, 1024, 512, 128
FLOPS = 2 * D * Q * (T + U)

F32 = mybir.dt.float32
BF16 = mybir.dt.bfloat16
I32 = mybir.dt.int32
U32 = mybir.dt.uint32
U16 = mybir.dt.uint16
U8 = mybir.dt.uint8
FP8X4 = mybir.dt.float8_e4m3fn_x4
FP4X4 = mybir.dt.float4_e2m1fn_x4
COPY = mybir.ActivationFunctionType.Copy
ALU = mybir.AluOpType

P = 128
PACK = 4
LIST_COLS = SLOTS // 16
HALF = SLOTS // 2
A_WIDTHS = (256, 256, 256, 128, 128)
B_COLS = 512
CAST_SPLIT = 22


def tile_attend_mutualput_two_kernel(
    tc, query, cache_words, cache_scales, draft_words, draft_scales, offs, offs2, offs3, offs4, offs5, out
):
    nc = tc.nc
    with ExitStack() as ctx:
        sb = ctx.enter_context(tc.tile_pool(name="sb", bufs=1))
        ps = ctx.enter_context(tc.psum_pool(name="ps", bufs=1))

        def load_list(source, name):
            tile = sb.tile([P, LIST_COLS], U16, name=name)
            nc.sync.dma_start(tile[:], source)
            return tile

        def half_of(list_tile, h):
            return list_tile[:, h * LIST_COLS // 2 : (h + 1) * LIST_COLS // 2]

        def load_scales(queue, plane, source):
            rows = source[0].bitcast(I32)
            for quadrant in range(4):
                queue.dma_start(
                    plane[32 * quadrant : 32 * quadrant + 4, :].bitcast(I32), rows[4 * quadrant : 4 * quadrant + 4, :]
                )

        cache_plane = sb.tile([P, T], U8, align_bytes=64)
        draft_plane = sb.tile([P, U], U8, align_bytes=64)
        nc.vector.memset(cache_plane[:].bitcast(I32), 0)

        q_raw = sb.tile([P, PACK, Q], F32)
        nc.sync.dma_start(q_raw[:], query.rearrange("(p j) q -> p j q", j=PACK))
        load_scales(nc.sync, cache_plane, cache_scales)
        cache_halves = []
        for h in range(2):
            codes = sb.tile([P, T], U8, align_bytes=64, name=f"cache_codes{h}")
            nc.sync.dma_start(codes[:].bitcast(I32), cache_words[0][:, h * T : (h + 1) * T].bitcast(I32))
            cache_halves.append(codes)
        draft_codes = sb.tile([P, U], U32, align_bytes=64, tag="draft_then_f3")
        nc.sync.dma_start(draft_codes[:].bitcast(I32), draft_words[0].rearrange("p n t -> p (n t)").bitcast(I32))
        idx = load_list(offs, "idx")
        idx2 = load_list(offs2, "idx2")
        nc.vector.memset(draft_plane[:].bitcast(I32), 0)
        load_scales(nc.sync, draft_plane, draft_scales)
        idx4 = load_list(offs4, "idx4")
        idx3 = load_list(offs3, "idx3")
        idx5 = load_list(offs5, "idx5")

        f1 = sb.tile([P, U], F32)
        f2 = sb.tile([P, T], F32)
        for window in (f1, f2):
            nc.vector.memset(window[:].bitcast(I32), 0)

        q_bf = sb.tile([P, Q, PACK], BF16, align_bytes=64)
        woven = q_bf[:].rearrange("p (c i) j -> p c j i", i=4)
        planar = q_raw[:].rearrange("p j (c i) -> p c j i", i=4)
        nc.vector.tensor_copy(woven[:, 0:CAST_SPLIT], planar[:, 0:CAST_SPLIT])
        nc.scalar.activation(woven[:, CAST_SPLIT:], planar[:, CAST_SPLIT:], COPY)
        q_codes = sb.tile([P, Q], U32, align_bytes=64)
        q_plane = sb.tile([P, Q], U8, align_bytes=64)
        nc.vector.quantize_mx(q_codes[:].bitcast(FP8X4), q_plane[:], q_bf[:].rearrange("p q j -> p (q j)"))

        a = sb.tile([P, T], F32)
        for piece, width in enumerate(A_WIDTHS):
            cols = slice(sum(A_WIDTHS[:piece]), sum(A_WIDTHS[: piece + 1]))
            bank = ps.tile([P, width], F32, name=f"a_bank{piece}")
            nc.tensor.matmul_mx(
                bank[:],
                lhsT=q_codes[:].bitcast(FP8X4),
                lhsT_scale=q_plane[:],
                rhs=cache_halves[cols.start // 512][:, 2 * (cols.start % 512) : 2 * (cols.start % 512 + width)].bitcast(FP4X4),
                rhs_scale=cache_plane[:, cols],
                start=True,
                stop=True,
            )
            if piece % 2 == 0:
                nc.scalar.activation(a[:, cols], bank[:], COPY)
            else:
                nc.vector.tensor_copy(a[:, cols], bank[:])

        picked_a = sb.tile([P, SLOTS], F32)
        nc.vector.tensor_copy(picked_a[:, 0:HALF], a[:].indirect(half_of(idx, 0)))
        nc.scalar.activation(picked_a[:, HALF:SLOTS], a[:].indirect(half_of(idx, 1)), COPY)
        nc.scalar.activation(f1[:].indirect(idx2[:]), picked_a[:], COPY)

        b = sb.tile([P, U], F32)
        for piece in range(U // B_COLS):
            cols = slice(piece * B_COLS, (piece + 1) * B_COLS)
            bank = ps.tile([P, B_COLS], F32, name=f"b_bank{piece}")
            nc.tensor.matmul_mx(
                bank[:],
                lhsT=q_codes[:].bitcast(FP8X4),
                lhsT_scale=q_plane[:],
                rhs=draft_codes[:, cols].bitcast(FP8X4),
                rhs_scale=draft_plane[:, cols],
                start=True,
                stop=True,
            )
            nc.vector.tensor_copy(b[:, cols], bank[:])

        picked_b = sb.tile([P, SLOTS], F32)
        nc.vector.tensor_copy(picked_b[:], b[:].indirect(idx2[:]))
        nc.scalar.activation(f2[:].indirect(idx[:]), picked_b[:], COPY)

        f3 = sb.tile([P, T], F32, align_bytes=64, tag="draft_then_f3")
        nc.gpsimd.memset(f3[:].bitcast(I32), 0)
        bb = sb.tile([P, U], F32, tag="bb_then_aa")
        nc.vector.tensor_tensor(bb[:], b[:], f1[:], ALU.subtract)
        picked_bb = sb.tile([P, SLOTS], F32)
        nc.vector.tensor_copy(picked_bb[:], bb[:].indirect(idx4[:]))
        nc.scalar.activation(f3[:].indirect(idx3[:]), picked_bb[:], COPY)

        aa = sb.tile([P, T], F32, tag="bb_then_aa")
        nc.vector.tensor_tensor(aa[:], a[:], f2[:], ALU.max)
        ac = sb.tile([P, T], F32)
        nc.vector.tensor_tensor(ac[:], aa[:], f3[:], ALU.add)

        y0 = sb.tile([P, HALF], F32)
        nc.vector.tensor_copy(y0[:], ac[:].indirect(half_of(idx5, 0)))
        nc.sync.dma_start(out[:, 0:HALF], y0[:])
        y1 = sb.tile([P, HALF], F32)
        nc.scalar.activation(y1[:], ac[:].indirect(half_of(idx5, 1)), COPY)
        nc.scalar.dma_start(out[:, HALF:SLOTS], y1[:])
